import numpy as np
import ml_dtypes


def mxq(x, axis, fmt="e4m3"):
    dtype, down = {"e4m3": (ml_dtypes.float8_e4m3fn, 7), "e5m2": (ml_dtypes.float8_e5m2, 14)}[fmt]
    v = np.moveaxis(np.asarray(x, np.float32).astype(ml_dtypes.bfloat16).astype(np.float64), axis, -1)
    blocks = v.reshape(v.shape[:-1] + (-1, 32))
    amax = np.abs(blocks).max(-1, keepdims=True)
    byte = np.maximum(np.where(amax > 0, np.frexp(amax)[1] - 1 + 127, 0) - down, 1)
    scale = np.exp2(byte - 127.0)
    codes = (blocks / scale).astype(np.float32).astype(dtype).astype(np.float64)
    return np.moveaxis((codes * scale).reshape(v.shape), -1, axis)


WIDE = False


def mx_kscale(k):
    if not WIDE:
        return np.ones(k)
    levels = np.array([10, -10, 5, -5, 0])
    if k % 512:
        return np.exp2(np.random.permutation(np.resize(levels, k // 32))).repeat(32)
    a = np.empty((k // 512, 16))
    for p in range(k // 512):
        a[p, :8] = np.random.permutation(np.resize(levels, 8))
        for g in range(8):
            far = levels[np.abs(levels - a[p, g]) >= 10]
            a[p, g + 8] = far[np.random.randint(len(far))]
    return np.exp2(a.ravel()).repeat(32)


def f64(x):
    return np.asarray(x).astype(np.float64)


def striped(idx):
    return np.tile(idx.reshape(-1, 16).T, (8, 1)).astype(np.uint16)


def unstriped(offs):
    return offs[:16].T.reshape(-1).astype(np.int64)


def striped8(idx):
    return np.concatenate([x.reshape(-1, 16).T for x in idx]).astype(np.uint16)


def runs(offs, k):
    lists = np.stack([offs[16 * r : 16 * r + 16].T.reshape(-1) for r in range(8)]).astype(np.int64)
    return lists[np.arange(k) % 512 // 64]


def pack_weight(w):
    k, n = w.shape
    w = f64(np.asarray(w, np.float32).astype(ml_dtypes.bfloat16)).reshape(k // 32, 32, n)
    amax = np.abs(w).max(1)
    byte = np.clip(np.where(amax > 0, np.frexp(amax)[1] - 1 + 127 - 7, 1), 1, 254)
    scaled = (w * np.exp2(127.0 - byte)[:, None, :]).reshape(k, n).astype(np.float32)
    words = np.ascontiguousarray(scaled.reshape(k // 512, 128, 4, n).transpose(0, 1, 3, 2)).astype(ml_dtypes.float8_e4m3fn).view(np.uint8)
    return words, np.ascontiguousarray(byte.astype(np.uint8).reshape(k // 512, 16, n))


def unpack_weight(words, scales):
    g, p, n, _ = words.shape
    vals = np.ascontiguousarray(words).view(ml_dtypes.float8_e4m3fn).astype(np.float64) * np.repeat(np.exp2(scales.astype(np.float64) - 127.0), 8, axis=1)[..., None]
    return vals.transpose(0, 1, 3, 2).reshape(g * 512, n)


K, T, S, G, H, J = 512, 2048, 512, 2048, 512, 512


def setup_inputs():
    n = np.random.standard_normal
    s = mx_kscale(K)[:, None]
    packed_xT = pack_weight(n((K, T)) * s)
    packed_dT = pack_weight(n((K, G)) / s)
    return {
        "x_words": packed_xT[0],
        "x_scales": packed_xT[1],
        "d_words": packed_dT[0],
        "d_scales": packed_dT[1],
        "gs": (np.random.uniform(0.5, 1.5, (K, 1)) * s).astype(np.float32),
        "tab": n((H, J)).astype(np.float32),
        "offs": striped(np.random.permutation(T)[:S]),
        "k1": striped8(np.random.randint(0, G, (8, H))),
        "n1": striped8(np.stack([np.random.permutation(S) for _ in range(8)])),
        "n2": striped8(np.stack([np.random.permutation(S) for _ in range(8)])),
        "n3": striped8(np.random.randint(0, J, (8, S))),
        "n4": striped8(np.stack([np.random.permutation(S) for _ in range(8)])),
    }


def reference(x_words, x_scales, d_words, d_scales, gs, tab, offs, k1, n1, n2, n3, n4):
    d_k1 = unpack_weight(d_words, d_scales)[np.arange(K)[:, None], runs(k1, K)]
    xq = unpack_weight(x_words, x_scales)[:, unstriped(offs)]
    h = 0.0625 * (d_k1.T @ xq)
    z = f64(gs) * ((np.tanh(h[np.arange(H)[:, None], runs(n1, H)] - h)) * (h[np.arange(H)[:, None], runs(n2, H)]))
    h2 = 0.0625 * ((d_k1.T @ mxq(z, 0, "e4m3")))
    return np.abs(h2 - (h2[np.arange(H)[:, None], runs(n4, H)]) - (f64(tab)[np.arange(H)[:, None], runs(n3, H)]))

@@ -1,0 +1,174 @@
+from contextlib import ExitStack
+
+import concourse.mybir as mybir
+
+K, T, S, G, H, J = 512, 2048, 512, 2048, 512, 512
+FLOPS = 2 * 2 * K * H * S
+
+F32 = mybir.dt.float32
+BF16 = mybir.dt.bfloat16
+I32 = mybir.dt.int32
+U32 = mybir.dt.uint32
+U16 = mybir.dt.uint16
+U8 = mybir.dt.uint8
+FP8X4 = mybir.dt.float8_e4m3fn_x4
+ALU = mybir.AluOpType
+ACT = mybir.ActivationFunctionType
+
+P = 128
+PACK = 4
+SIXTEENTH = 0.0625
+PIECES = ((0, 256), (256, 512))
+SHIFT = 14
+MOVED = 112
+
+
+def tile_picked_ringfdifkindd_none_p_kernel(tc, x_words, x_scales, d_words, d_scales, gs, tab, offs, k1, n1, n2, n3, n4, out):
+    nc = tc.nc
+    with ExitStack() as ctx:
+        lists = ctx.enter_context(tc.tile_pool(name="lists", bufs=1))
+        sb = ctx.enter_context(tc.tile_pool(name="sb", bufs=1))
+        ps = ctx.enter_context(tc.psum_pool(name="ps", bufs=1))
+
+        def load_list(src, name):
+            tile = lists.tile([P, S // 16], U16, name=name)
+            nc.sync.dma_start(tile[:], src)
+            return tile
+
+        def entries(tile, lo, hi):
+            return tile[:, lo // 16 : hi // 16]
+
+        xs_win = sb.tile([P, T], U8, name="xs_win", align_bytes=64)
+        ds_plane = sb.tile([P, H], U8, name="ds_plane", align_bytes=64)
+        nc.vector.memset(xs_win[:].bitcast(I32), 0)
+        nc.gpsimd.memset(ds_plane[:].bitcast(I32), 0)
+
+        k1_t = load_list(k1, "k1_t")
+        ds_win = sb.tile([P, G], U8, name="ds_win", align_bytes=64)
+        ds_rows = d_scales[0].bitcast(I32)
+        for b in range(2):
+            nc.sync.dma_start(
+                ds_win[:].bitcast(I32)[b:P:2, :],
+                ds_rows[b:16:2, :].unsqueeze(1).broadcast_to([8, 8, G // 4]),
+            )
+        gs_t = sb.tile([P, PACK], F32, name="gs_t")
+        nc.scalar.dma_start(gs_t[:], gs.rearrange("(p t) o -> p (t o)", t=PACK))
+        xs_rows = x_scales[0].bitcast(I32)
+        for q in range(4):
+            nc.scalar.dma_start(xs_win[:].bitcast(I32)[32 * q : 32 * q + 4, :], xs_rows[4 * q : 4 * q + 4, :])
+        dw_win = sb.tile([P, G], I32, name="dw_win", align_bytes=64)
+        nc.sync.dma_start(dw_win[:], d_words[0].rearrange("p n t -> p (n t)").bitcast(I32))
+        offs_t = load_list(offs, "offs_t")
+        xw_win = sb.tile([P, T], I32, name="xw_win", align_bytes=64)
+        nc.sync.dma_start(xw_win[:], x_words[0].rearrange("p n t -> p (n t)").bitcast(I32))
+        n1_t = load_list(n1, "n1_t")
+        n2_t = load_list(n2, "n2_t")
+        n3_t = load_list(n3, "n3_t")
+        tab_rows = tab.rearrange("(p t) j -> p t j", t=PACK)
+        tab_win = []
+        for t in range(PACK):
+            tile = sb.tile([P, J], F32, name="tab_win%d" % t)
+            nc.sync.dma_start(tile[:], tab_rows[:, t, :])
+            tab_win.append(tile)
+        n4_t = load_list(n4, "n4_t")
+
+        gs16 = sb.tile([P, PACK], F32, name="gs16")
+        nc.scalar.activation(gs16[:], gs_t[:], ACT.Copy, scale=SIXTEENTH)
+        gs_safe = sb.tile([P, PACK], F32, name="gs_safe")
+        gs_inv = sb.tile([P, PACK], F32, name="gs_inv")
+
+        ds_got = sb.tile([P, H], U8, name="ds_got", align_bytes=64)
+        nc.vector.tensor_copy(ds_got[:], ds_win[:].indirect(k1_t[:]))
+        ds_dealt = sb.tile([P, H], U8, name="ds_dealt", align_bytes=64)
+        nc.vector.tensor_copy(
+            ds_dealt[:].rearrange("p (t c i) -> p c t i", t=PACK, i=16),
+            ds_got[:].rearrange("p (c i t) -> p c t i", t=PACK, i=16),
+        )
+        nc.scalar.dma_start(
+            ds_plane[:].bitcast(I32)[0:MOVED, :], ds_dealt[:].bitcast(I32)[SHIFT : SHIFT + MOVED, :]
+        )
+        nc.vector.scalar_tensor_tensor(gs_safe[:], gs_t[:], 0.0, gs_t[:], ALU.is_equal, ALU.subtract)
+        nc.vector.reciprocal(gs_inv[:], gs_safe[:])
+
+        dw_got = sb.tile([P, H], I32, name="dw_got", align_bytes=64)
+        nc.vector.tensor_copy(dw_got[:].bitcast(U32), dw_win[:].bitcast(U32).indirect(k1_t[:]))
+        dw_dealt = sb.tile([P, H], I32, name="dw_dealt", align_bytes=64)
+        nc.vector.tensor_copy(
+            dw_dealt[:].rearrange("p (t c i) -> p c t i", t=PACK, i=4),
+            dw_got[:].rearrange("p (c i t) -> p c t i", t=PACK, i=4),
+        )
+        xs_got = sb.tile([P, S], U8, name="xs_got", align_bytes=64)
+        nc.vector.tensor_copy(xs_got[:], xs_win[:].indirect(offs_t[:]))
+        xw_got = sb.tile([P, S], I32, name="xw_got", align_bytes=64)
+        nc.vector.tensor_copy(xw_got[:].bitcast(U32), xw_win[:].bitcast(U32).indirect(offs_t[:]))
+
+        def product(bank, t, codes, scales):
+            rows = slice(t * P, (t + 1) * P)
+            nc.tensor.matmul_mx(
+                out=bank,
+                lhsT=dw_dealt[:, rows].bitcast(FP8X4),
+                lhsT_scale=ds_plane[:, rows],
+                rhs=codes.bitcast(FP8X4),
+                rhs_scale=scales,
+                start=True,
+                stop=True,
+            )
+
+        gh, h_bank = [], []
+        for t in range(PACK):
+            bank = ps.tile([P, S], F32, name="h_bank%d" % t)
+            product(bank[:], t, xw_got[:], xs_got[:])
+            tile = sb.tile([P, S], F32, name="gh%d" % t)
+            nc.scalar.activation(tile[:], bank[:], ACT.Copy, scale=gs16[:, t : t + 1])
+            gh.append(tile)
+            h_bank.append(bank)
+
+        h2_bank = [ps.tile([P, S], F32, name="h2_bank%d" % t) for t in range(PACK)]
+        h2 = [sb.tile([P, S], F32, name="h2_%d" % t) for t in range(PACK)]
+        kinds = [sb.tile([P, S], F32, name="kinds%d" % t) for t in range(PACK)]
+        rest = [sb.tile([P, S], F32, name="rest%d" % t) for t in range(PACK)]
+        near, diff, bend, other = {}, {}, {}, {}
+        for lo, hi in PIECES:
+            n = hi - lo
+            near[lo] = sb.tile([P, PACK, n], F32, name="near%d" % lo)
+            diff[lo] = sb.tile([P, PACK, n], F32, name="diff%d" % lo)
+            bend[lo] = sb.tile([P, PACK, n], F32, name="bend%d" % lo)
+            other[lo] = sb.tile([P, PACK, n], F32, name="other%d" % lo)
+            for t in range(PACK):
+                nc.scalar.activation(near[lo][:, t, :], gh[t][:].indirect(entries(n1_t, lo, hi)), ACT.Copy)
+                nc.vector.tensor_copy(other[lo][:, t, :], gh[t][:].indirect(entries(n2_t, lo, hi)))
+                nc.vector.scalar_tensor_tensor(
+                    diff[lo][:, t, :], h_bank[t][:, lo:hi], gs16[:, t : t + 1], near[lo][:, t, :], ALU.mult, ALU.subtract
+                )
+                nc.scalar.activation(bend[lo][:, t, :], diff[lo][:, t, :], ACT.Tanh, scale=gs_inv[:, t : t + 1])
+        for lo, hi in PIECES:
+            n = hi - lo
+            z = sb.tile([P, n, PACK], BF16, name="z%d" % lo, align_bytes=64)
+            nc.vector.tensor_tensor(
+                z[:].rearrange("p (c i) t -> p c t i", i=4),
+                bend[lo][:].rearrange("p t (c i) -> p c t i", i=4),
+                other[lo][:].rearrange("p t (c i) -> p c t i", i=4),
+                ALU.mult,
+            )
+            z_codes = sb.tile([P, n], U32, name="z_codes%d" % lo, align_bytes=64)
+            z_scales = sb.tile([P, n], U8, name="z_scales%d" % lo, align_bytes=64)
+            nc.vector.quantize_mx(
+                out=z_codes[:].bitcast(FP8X4), scales=z_scales[:], in_=z[:].rearrange("p c t -> p (c t)")
+            )
+            for t in range(PACK):
+                product(h2_bank[t][:, lo:hi], t, z_codes[:], z_scales[:])
+                nc.scalar.activation(h2[t][:, lo:hi], h2_bank[t][:, lo:hi], ACT.Copy, scale=SIXTEENTH)
+            for t in range(PACK):
+                nc.scalar.activation(kinds[t][:, lo:hi], tab_win[t][:].indirect(entries(n3_t, lo, hi)), ACT.Copy)
+                nc.vector.tensor_tensor(rest[t][:, lo:hi], kinds[t][:, lo:hi], h2[t][:, lo:hi], ALU.subtract)
+
+        out_rows = out.rearrange("(p t) j -> p t j", t=PACK)
+        for t in range(PACK):
+            total = sb.tile([P, S], F32, name="total%d" % t)
+            size = sb.tile([P, S], F32, name="size%d" % t)
+            for lo, hi in PIECES:
+                nc.vector.tensor_tensor(
+                    total[:, lo:hi], h2[t][:].indirect(entries(n4_t, lo, hi)), rest[t][:, lo:hi], ALU.add
+                )
+                nc.scalar.activation(size[:, lo:hi], total[:, lo:hi], ACT.Abs)
+                nc.sync.dma_start(out_rows[:, t, lo:hi], size[:, lo:hi])

@@ -18,9 +18,8 @@ ACT = mybir.ActivationFunctionType
 P = 128
 PACK = 4
 SIXTEENTH = 0.0625
-PIECES = ((0, 256), (256, 512))
-SHIFT = 14
-MOVED = 112
+HALF = S // 2
+HALVES = (slice(0, HALF), slice(HALF, S))
 
 
 def tile_picked_ringfdifkindd_none_p_kernel(tc, x_words, x_scales, d_words, d_scales, gs, tab, offs, k1, n1, n2, n3, n4, out):
@@ -35,72 +34,75 @@ def tile_picked_ringfdifkindd_none_p_kernel(tc, x_words, x_scales, d_words, d_sc
             nc.sync.dma_start(tile[:], src)
             return tile
 
-        def entries(tile, lo, hi):
-            return tile[:, lo // 16 : hi // 16]
+        def entries(tile, cols):
+            return tile[:, cols.start // 16 : cols.stop // 16]
 
-        xs_win = sb.tile([P, T], U8, name="xs_win", align_bytes=64)
-        ds_plane = sb.tile([P, H], U8, name="ds_plane", align_bytes=64)
+        def sbuf(shape, dtype, name, tag=None):
+            return sb.tile(shape, dtype, name=name, tag=tag or name, align_bytes=64)
+
+        xs_win = sbuf([P, T], U8, "xs_win")
+        ds_plane = sbuf([P, H], U8, "ds_plane")
         nc.vector.memset(xs_win[:].bitcast(I32), 0)
         nc.gpsimd.memset(ds_plane[:].bitcast(I32), 0)
 
         k1_t = load_list(k1, "k1_t")
-        ds_win = sb.tile([P, G], U8, name="ds_win", align_bytes=64)
-        ds_rows = d_scales[0].bitcast(I32)
-        for b in range(2):
-            nc.sync.dma_start(
-                ds_win[:].bitcast(I32)[b:P:2, :],
-                ds_rows[b:16:2, :].unsqueeze(1).broadcast_to([8, 8, G // 4]),
-            )
-        gs_t = sb.tile([P, PACK], F32, name="gs_t")
+        ds_win = sbuf([P, G], U8, "ds_win")
+        nc.sync.dma_start(
+            ds_win[:].bitcast(I32), d_scales[0].bitcast(I32).unsqueeze(1).broadcast_to([16, 8, G // 4])
+        )
+        gs_t = sbuf([P, PACK], F32, "gs_t")
         nc.scalar.dma_start(gs_t[:], gs.rearrange("(p t) o -> p (t o)", t=PACK))
         xs_rows = x_scales[0].bitcast(I32)
         for q in range(4):
             nc.scalar.dma_start(xs_win[:].bitcast(I32)[32 * q : 32 * q + 4, :], xs_rows[4 * q : 4 * q + 4, :])
-        dw_win = sb.tile([P, G], I32, name="dw_win", align_bytes=64)
+        dw_win = sbuf([P, G], I32, "dw_win")
         nc.sync.dma_start(dw_win[:], d_words[0].rearrange("p n t -> p (n t)").bitcast(I32))
         offs_t = load_list(offs, "offs_t")
-        xw_win = sb.tile([P, T], I32, name="xw_win", align_bytes=64)
+        xw_win = sbuf([P, T], I32, "xw_win")
         nc.sync.dma_start(xw_win[:], x_words[0].rearrange("p n t -> p (n t)").bitcast(I32))
         n1_t = load_list(n1, "n1_t")
         n2_t = load_list(n2, "n2_t")
         n3_t = load_list(n3, "n3_t")
-        tab_rows = tab.rearrange("(p t) j -> p t j", t=PACK)
-        tab_win = []
-        for t in range(PACK):
-            tile = sb.tile([P, J], F32, name="tab_win%d" % t)
-            nc.sync.dma_start(tile[:], tab_rows[:, t, :])
-            tab_win.append(tile)
         n4_t = load_list(n4, "n4_t")
 
-        gs16 = sb.tile([P, PACK], F32, name="gs16")
+        gs16 = sbuf([P, PACK], F32, "gs16")
         nc.scalar.activation(gs16[:], gs_t[:], ACT.Copy, scale=SIXTEENTH)
-        gs_safe = sb.tile([P, PACK], F32, name="gs_safe")
-        gs_inv = sb.tile([P, PACK], F32, name="gs_inv")
+        gs_safe = sbuf([P, PACK], F32, "gs_safe")
+        gs_inv = sbuf([P, PACK], F32, "gs_inv")
 
-        ds_got = sb.tile([P, H], U8, name="ds_got", align_bytes=64)
+        ds_got = sbuf([P, H], U8, "ds_got")
         nc.vector.tensor_copy(ds_got[:], ds_win[:].indirect(k1_t[:]))
-        ds_dealt = sb.tile([P, H], U8, name="ds_dealt", align_bytes=64)
+        ds_dealt = sbuf([P, H], U8, "ds_dealt")
         nc.vector.tensor_copy(
             ds_dealt[:].rearrange("p (t c i) -> p c t i", t=PACK, i=16),
             ds_got[:].rearrange("p (c i t) -> p c t i", t=PACK, i=16),
         )
-        nc.scalar.dma_start(
-            ds_plane[:].bitcast(I32)[0:MOVED, :], ds_dealt[:].bitcast(I32)[SHIFT : SHIFT + MOVED, :]
-        )
+        for a in range(4):
+            nc.scalar.dma_start(ds_plane[:].bitcast(I32)[a:P:32, :], ds_dealt[:].bitcast(I32)[8 * a : P : 32, :])
         nc.vector.scalar_tensor_tensor(gs_safe[:], gs_t[:], 0.0, gs_t[:], ALU.is_equal, ALU.subtract)
         nc.vector.reciprocal(gs_inv[:], gs_safe[:])
 
-        dw_got = sb.tile([P, H], I32, name="dw_got", align_bytes=64)
+        dw_got = sbuf([P, H], I32, "dw_got")
         nc.vector.tensor_copy(dw_got[:].bitcast(U32), dw_win[:].bitcast(U32).indirect(k1_t[:]))
-        dw_dealt = sb.tile([P, H], I32, name="dw_dealt", align_bytes=64)
+        dw_dealt = sbuf([P, H], I32, "dw_dealt")
         nc.vector.tensor_copy(
             dw_dealt[:].rearrange("p (t c i) -> p c t i", t=PACK, i=4),
             dw_got[:].rearrange("p (c i t) -> p c t i", t=PACK, i=4),
         )
-        xs_got = sb.tile([P, S], U8, name="xs_got", align_bytes=64)
+        xs_got = sbuf([P, S], U8, "xs_got")
         nc.vector.tensor_copy(xs_got[:], xs_win[:].indirect(offs_t[:]))
-        xw_got = sb.tile([P, S], I32, name="xw_got", align_bytes=64)
-        nc.vector.tensor_copy(xw_got[:].bitcast(U32), xw_win[:].bitcast(U32).indirect(offs_t[:]))
+        xw_got = sbuf([P, S], I32, "xw_got")
+        for cols in HALVES:
+            nc.vector.tensor_copy(
+                xw_got[:, cols].bitcast(U32), xw_win[:].bitcast(U32).indirect(entries(offs_t, cols))
+            )
+
+        tab_rows = tab.rearrange("(p t) j -> p t j", t=PACK)
+        tab_win = []
+        for t, slot in enumerate(("ds_got", "dw_got", "xs_win", "xw_win")):
+            tile = sbuf([P, J], F32, "tab_win%d" % t, tag=slot)
+            nc.sync.dma_start(tile[:], tab_rows[:, t, :])
+            tab_win.append(tile)
 
         def product(bank, t, codes, scales):
             rows = slice(t * P, (t + 1) * P)
@@ -114,61 +116,94 @@ def tile_picked_ringfdifkindd_none_p_kernel(tc, x_words, x_scales, d_words, d_sc
                 stop=True,
             )
 
-        gh, h_bank = [], []
+        banks = [[ps.tile([P, HALF], F32, name="bank%d%d" % (t, u)) for u in range(2)] for t in range(PACK)]
+        rows_win = [sbuf([P, 2 * S], F32, "rows_win%d" % t) for t in range(PACK)]
         for t in range(PACK):
-            bank = ps.tile([P, S], F32, name="h_bank%d" % t)
-            product(bank[:], t, xw_got[:], xs_got[:])
-            tile = sb.tile([P, S], F32, name="gh%d" % t)
-            nc.scalar.activation(tile[:], bank[:], ACT.Copy, scale=gs16[:, t : t + 1])
-            gh.append(tile)
-            h_bank.append(bank)
+            nc.gpsimd.memset(rows_win[t][:, S:], 0.0)
 
-        h2_bank = [ps.tile([P, S], F32, name="h2_bank%d" % t) for t in range(PACK)]
-        h2 = [sb.tile([P, S], F32, name="h2_%d" % t) for t in range(PACK)]
-        kinds = [sb.tile([P, S], F32, name="kinds%d" % t) for t in range(PACK)]
-        rest = [sb.tile([P, S], F32, name="rest%d" % t) for t in range(PACK)]
-        near, diff, bend, other = {}, {}, {}, {}
-        for lo, hi in PIECES:
-            n = hi - lo
-            near[lo] = sb.tile([P, PACK, n], F32, name="near%d" % lo)
-            diff[lo] = sb.tile([P, PACK, n], F32, name="diff%d" % lo)
-            bend[lo] = sb.tile([P, PACK, n], F32, name="bend%d" % lo)
-            other[lo] = sb.tile([P, PACK, n], F32, name="other%d" % lo)
+        for pair in ((0, 1), (2, 3)):
+            for u, cols in enumerate(HALVES):
+                for t in pair:
+                    product(banks[t][u][:], t, xw_got[:, cols], xs_got[:, cols])
+                    nc.scalar.activation(rows_win[t][:, cols], banks[t][u][:], ACT.Copy, scale=gs16[:, t : t + 1])
+
+        near = sbuf([P, 2, HALF], F32, "near")
+        diff = [sbuf([P, PACK, HALF], F32, "diff%d" % u) for u in range(2)]
+        bend = [sbuf([P, PACK, HALF], F32, "bend%d" % u) for u in range(2)]
+        other = [sbuf([P, PACK, HALF], F32, "other%d" % u) for u in range(2)]
+        for u, cols in enumerate(HALVES):
             for t in range(PACK):
-                nc.scalar.activation(near[lo][:, t, :], gh[t][:].indirect(entries(n1_t, lo, hi)), ACT.Copy)
-                nc.vector.tensor_copy(other[lo][:, t, :], gh[t][:].indirect(entries(n2_t, lo, hi)))
+                nc.vector.tensor_copy(near[:, t % 2, :], rows_win[t][:].indirect(entries(n1_t, cols)))
                 nc.vector.scalar_tensor_tensor(
-                    diff[lo][:, t, :], h_bank[t][:, lo:hi], gs16[:, t : t + 1], near[lo][:, t, :], ALU.mult, ALU.subtract
+                    diff[u][:, t, :], banks[t][u][:], gs16[:, t : t + 1], near[:, t % 2, :], ALU.mult, ALU.subtract
                 )
-                nc.scalar.activation(bend[lo][:, t, :], diff[lo][:, t, :], ACT.Tanh, scale=gs_inv[:, t : t + 1])
-        for lo, hi in PIECES:
-            n = hi - lo
-            z = sb.tile([P, n, PACK], BF16, name="z%d" % lo, align_bytes=64)
+                nc.scalar.activation(other[u][:, t, :], rows_win[t][:].indirect(entries(n2_t, cols)), ACT.Copy)
+                nc.scalar.activation(bend[u][:, t, :], diff[u][:, t, :], ACT.Tanh, scale=gs_inv[:, t : t + 1])
+
+        def fetch_kinds(t, u, into):
+            nc.scalar.activation(into, tab_win[t][:].indirect(entries(n3_t, HALVES[u])), ACT.Copy)
+
+        kinds1 = (diff[1][:, 3, :], other[1][:, 0, :])
+        for u, cols in enumerate(HALVES):
+            z = sbuf([P, HALF, PACK], BF16, "z%d" % u, tag="near")
             nc.vector.tensor_tensor(
                 z[:].rearrange("p (c i) t -> p c t i", i=4),
-                bend[lo][:].rearrange("p t (c i) -> p c t i", i=4),
-                other[lo][:].rearrange("p t (c i) -> p c t i", i=4),
+                bend[u][:].rearrange("p t (c i) -> p c t i", i=4),
+                other[u][:].rearrange("p t (c i) -> p c t i", i=4),
                 ALU.mult,
             )
-            z_codes = sb.tile([P, n], U32, name="z_codes%d" % lo, align_bytes=64)
-            z_scales = sb.tile([P, n], U8, name="z_scales%d" % lo, align_bytes=64)
+            z_codes = sbuf([P, HALF], U32, "z_codes%d" % u)
+            z_scales = sbuf([P, HALF], U8, "z_scales%d" % u)
             nc.vector.quantize_mx(
                 out=z_codes[:].bitcast(FP8X4), scales=z_scales[:], in_=z[:].rearrange("p c t -> p (c t)")
             )
+            fetch_kinds(1, u, kinds1[u])
             for t in range(PACK):
-                product(h2_bank[t][:, lo:hi], t, z_codes[:], z_scales[:])
-                nc.scalar.activation(h2[t][:, lo:hi], h2_bank[t][:, lo:hi], ACT.Copy, scale=SIXTEENTH)
-            for t in range(PACK):
-                nc.scalar.activation(kinds[t][:, lo:hi], tab_win[t][:].indirect(entries(n3_t, lo, hi)), ACT.Copy)
-                nc.vector.tensor_tensor(rest[t][:, lo:hi], kinds[t][:, lo:hi], h2[t][:, lo:hi], ALU.subtract)
+                product(banks[t][u][:], t, z_codes[:], z_scales[:])
+                nc.scalar.activation(rows_win[t][:, cols], banks[t][u][:], ACT.Copy, scale=SIXTEENTH)
 
+        first, second = HALVES
+        whole = slice(0, S)
+        kinds0 = sbuf([P, S], F32, "kinds0")
+        rest = [sbuf([P, S], F32, "rest%d" % t) for t in range(PACK)]
+        total = [sbuf([P, S], F32, "total%d" % t) for t in range(PACK)]
+        size = [sbuf([P, S], F32, "size%d" % t) for t in range(PACK)]
         out_rows = out.rearrange("(p t) j -> p t j", t=PACK)
-        for t in range(PACK):
-            total = sb.tile([P, S], F32, name="total%d" % t)
-            size = sb.tile([P, S], F32, name="size%d" % t)
-            for lo, hi in PIECES:
-                nc.vector.tensor_tensor(
-                    total[:, lo:hi], h2[t][:].indirect(entries(n4_t, lo, hi)), rest[t][:, lo:hi], ALU.add
-                )
-                nc.scalar.activation(size[:, lo:hi], total[:, lo:hi], ACT.Abs)
-                nc.sync.dma_start(out_rows[:, t, lo:hi], size[:, lo:hi])
+
+        def less_h2(t, cols, kinds):
+            nc.vector.tensor_tensor(rest[t][:, cols], kinds, rows_win[t][:, cols], ALU.subtract)
+
+        def add_far(t, cols):
+            nc.vector.tensor_tensor(
+                total[t][:, cols], rows_win[t][:].indirect(entries(n4_t, cols)), rest[t][:, cols], ALU.add
+            )
+
+        def finish(t, cols):
+            nc.scalar.activation(size[t][:, cols], total[t][:, cols], ACT.Abs)
+            nc.sync.dma_start(out_rows[:, t, cols], size[t][:, cols])
+
+        for cols in HALVES:
+            nc.vector.tensor_copy(kinds0[:, cols], tab_win[0][:].indirect(entries(n3_t, cols)))
+        less_h2(0, first, kinds0[:, first])
+        less_h2(1, first, kinds1[0])
+        nc.vector.tensor_tensor(
+            rest[2][:, first], tab_win[2][:].indirect(entries(n3_t, first)), rows_win[2][:, first], ALU.subtract
+        )
+        less_h2(0, second, kinds0[:, second])
+        less_h2(1, second, kinds1[1])
+        fetch_kinds(2, 1, kinds0[:, second])
+        far2 = sbuf([P, S], F32, "far2")
+        nc.scalar.activation(far2[:], rows_win[2][:].indirect(n4_t[:]), ACT.Copy)
+        add_far(0, whole)
+        for u, cols in enumerate(HALVES):
+            fetch_kinds(3, u, rest[0][:, cols])
+        finish(0, whole)
+        less_h2(2, second, kinds0[:, second])
+        add_far(1, whole)
+        finish(1, whole)
+        nc.vector.tensor_tensor(total[2][:], far2[:], rest[2][:], ALU.add)
+        less_h2(3, whole, rest[0][:])
+        finish(2, whole)
+        for cols in HALVES:
+            add_far(3, cols)
+            finish(3, cols)

@@ -72,6 +72,7 @@ def tile_picked_ringfdifkindd_none_p_kernel(tc, x_words, x_scales, d_words, d_sc
 
         ds_got = sbuf([P, H], U8, "ds_got")
         nc.vector.tensor_copy(ds_got[:], ds_win[:].indirect(k1_t[:]))
+        nc.vector.scalar_tensor_tensor(gs_safe[:], gs_t[:], 0.0, gs_t[:], ALU.is_equal, ALU.subtract)
         ds_dealt = sbuf([P, H], U8, "ds_dealt")
         nc.vector.tensor_copy(
             ds_dealt[:].rearrange("p (t c i) -> p c t i", t=PACK, i=16),
@@ -79,7 +80,6 @@ def tile_picked_ringfdifkindd_none_p_kernel(tc, x_words, x_scales, d_words, d_sc
         )
         for a in range(4):
             nc.scalar.dma_start(ds_plane[:].bitcast(I32)[a:P:32, :], ds_dealt[:].bitcast(I32)[8 * a : P : 32, :])
-        nc.vector.scalar_tensor_tensor(gs_safe[:], gs_t[:], 0.0, gs_t[:], ALU.is_equal, ALU.subtract)
         nc.vector.reciprocal(gs_inv[:], gs_safe[:])
 
         dw_got = sbuf([P, H], I32, "dw_got")
@@ -116,51 +116,69 @@ def tile_picked_ringfdifkindd_none_p_kernel(tc, x_words, x_scales, d_words, d_sc
                 stop=True,
             )
 
-        banks = [[ps.tile([P, HALF], F32, name="bank%d%d" % (t, u)) for u in range(2)] for t in range(PACK)]
+        early, late = (0, 1), (2, 3)
+        banks = {(t, u): ps.tile([P, HALF], F32, name="bank%d%d" % (t, u))[:] for t in early for u in range(2)}
+        whole_bank = {t: ps.tile([P, S], F32, name="bank%d" % t) for t in late}
+        for t in late:
+            for u, cols in enumerate(HALVES):
+                banks[t, u] = whole_bank[t][:, cols]
         rows_win = [sbuf([P, 2 * S], F32, "rows_win%d" % t) for t in range(PACK)]
         for t in range(PACK):
             nc.gpsimd.memset(rows_win[t][:, S:], 0.0)
 
-        for pair in ((0, 1), (2, 3)):
-            for u, cols in enumerate(HALVES):
-                for t in pair:
-                    product(banks[t][u][:], t, xw_got[:, cols], xs_got[:, cols])
-                    nc.scalar.activation(rows_win[t][:, cols], banks[t][u][:], ACT.Copy, scale=gs16[:, t : t + 1])
+        for u, cols in enumerate(HALVES):
+            for t in early:
+                product(banks[t, u], t, xw_got[:, cols], xs_got[:, cols])
+                nc.scalar.activation(rows_win[t][:, cols], banks[t, u], ACT.Copy, scale=gs16[:, t : t + 1])
+        for t in late:
+            product(whole_bank[t][:], t, xw_got[:], xs_got[:])
+            nc.scalar.activation(rows_win[t][:, 0:S], whole_bank[t][:], ACT.Copy, scale=gs16[:, t : t + 1])
 
-        near = sbuf([P, 2, HALF], F32, "near")
+        near = sbuf([P, PACK, HALF], F32, "near")
         diff = [sbuf([P, PACK, HALF], F32, "diff%d" % u) for u in range(2)]
         bend = [sbuf([P, PACK, HALF], F32, "bend%d" % u) for u in range(2)]
         other = [sbuf([P, PACK, HALF], F32, "other%d" % u) for u in range(2)]
-        for u, cols in enumerate(HALVES):
-            for t in range(PACK):
-                nc.vector.tensor_copy(near[:, t % 2, :], rows_win[t][:].indirect(entries(n1_t, cols)))
-                nc.vector.scalar_tensor_tensor(
-                    diff[u][:, t, :], banks[t][u][:], gs16[:, t : t + 1], near[:, t % 2, :], ALU.mult, ALU.subtract
-                )
-                nc.scalar.activation(other[u][:, t, :], rows_win[t][:].indirect(entries(n2_t, cols)), ACT.Copy)
-                nc.scalar.activation(bend[u][:, t, :], diff[u][:, t, :], ACT.Tanh, scale=gs_inv[:, t : t + 1])
+        steps = [(u, t) for u in range(2) for t in range(PACK)]
+
+        def fetch_near(u, t):
+            nc.vector.tensor_copy(near[:, t, :], rows_win[t][:].indirect(entries(n1_t, HALVES[u])))
+
+        fetch_near(*steps[0])
+        for step, (u, t) in enumerate(steps):
+            if step + 1 < len(steps):
+                fetch_near(*steps[step + 1])
+            nc.vector.scalar_tensor_tensor(
+                diff[u][:, t, :], banks[t, u], gs16[:, t : t + 1], near[:, t, :], ALU.mult, ALU.subtract
+            )
+            nc.scalar.activation(other[u][:, t, :], rows_win[t][:].indirect(entries(n2_t, HALVES[u])), ACT.Copy)
+            nc.scalar.activation(bend[u][:, t, :], diff[u][:, t, :], ACT.Tanh, scale=gs_inv[:, t : t + 1])
 
         def fetch_kinds(t, u, into):
             nc.scalar.activation(into, tab_win[t][:].indirect(entries(n3_t, HALVES[u])), ACT.Copy)
 
         kinds1 = (diff[1][:, 3, :], other[1][:, 0, :])
         for u, cols in enumerate(HALVES):
-            z = sbuf([P, HALF, PACK], BF16, "z%d" % u, tag="near")
-            nc.vector.tensor_tensor(
-                z[:].rearrange("p (c i) t -> p c t i", i=4),
-                bend[u][:].rearrange("p t (c i) -> p c t i", i=4),
-                other[u][:].rearrange("p t (c i) -> p c t i", i=4),
-                ALU.mult,
-            )
+            z = sbuf([P, HALF, PACK], BF16, "z%d" % u, tag=("near", "z1")[u])
             z_codes = sbuf([P, HALF], U32, "z_codes%d" % u)
             z_scales = sbuf([P, HALF], U8, "z_scales%d" % u)
-            nc.vector.quantize_mx(
-                out=z_codes[:].bitcast(FP8X4), scales=z_scales[:], in_=z[:].rearrange("p c t -> p (c t)")
-            )
+            quarters = (slice(0, HALF // 2), slice(HALF // 2, HALF))
+            for part in quarters:
+                nc.vector.tensor_tensor(
+                    z[:, part, :].rearrange("p (c i) t -> p c t i", i=4),
+                    bend[u][:, :, part].rearrange("p t (c i) -> p c t i", i=4),
+                    other[u][:, :, part].rearrange("p t (c i) -> p c t i", i=4),
+                    ALU.mult,
+                )
+            for part in quarters:
+                nc.vector.quantize_mx(
+                    out=z_codes[:, part].bitcast(FP8X4),
+                    scales=z_scales[:, part],
+                    in_=z[:, part, :].rearrange("p c t -> p (c t)"),
+                )
             fetch_kinds(1, u, kinds1[u])
             for t in range(PACK):
-                product(banks[t][u][:], t, z_codes[:], z_scales[:])
-                nc.scalar.activation(rows_win[t][:, cols], banks[t][u][:], ACT.Copy, scale=SIXTEENTH)
+                product(banks[t, u], t, z_codes[:], z_scales[:])
+                nc.scalar.activation(rows_win[t][:, cols], banks[t, u], ACT.Copy, scale=SIXTEENTH)
 
         first, second = HALVES
         whole = slice(0, S)
@@ -192,17 +210,18 @@ def tile_picked_ringfdifkindd_none_p_kernel(tc, x_words, x_scales, d_words, d_sc
         less_h2(0, second, kinds0[:, second])
         less_h2(1, second, kinds1[1])
         fetch_kinds(2, 1, kinds0[:, second])
+        fetch_kinds(3, 0, kinds1[1])
+        add_far(0, whole)
+        fetch_kinds(3, 1, rest[0][:, first])
         far2 = sbuf([P, S], F32, "far2")
         nc.scalar.activation(far2[:], rows_win[2][:].indirect(n4_t[:]), ACT.Copy)
-        add_far(0, whole)
-        for u, cols in enumerate(HALVES):
-            fetch_kinds(3, u, rest[0][:, cols])
         finish(0, whole)
         less_h2(2, second, kinds0[:, second])
+        less_h2(3, first, kinds1[1])
         add_far(1, whole)
         finish(1, whole)
+        less_h2(3, second, rest[0][:, first])
         nc.vector.tensor_tensor(total[2][:], far2[:], rest[2][:], ALU.add)
-        less_h2(3, whole, rest[0][:])
         finish(2, whole)
         for cols in HALVES:
             add_far(3, cols)

@@ -42,7 +42,7 @@ def tile_picked_ringfdifkindd_none_p_kernel(tc, x_words, x_scales, d_words, d_sc
 
         xs_win = sbuf([P, T], U8, "xs_win")
         ds_plane = sbuf([P, H], U8, "ds_plane")
-        nc.vector.memset(xs_win[:].bitcast(I32), 0)
+        nc.gpsimd.memset(xs_win[:].bitcast(I32), 0)
         nc.gpsimd.memset(ds_plane[:].bitcast(I32), 0)
 
         k1_t = load_list(k1, "k1_t")

from contextlib import ExitStack

import concourse.mybir as mybir

K, T, S, G, H, J = 512, 2048, 512, 2048, 512, 512
FLOPS = 2 * 2 * K * H * S

F32 = mybir.dt.float32
BF16 = mybir.dt.bfloat16
I32 = mybir.dt.int32
U32 = mybir.dt.uint32
U16 = mybir.dt.uint16
U8 = mybir.dt.uint8
FP8X4 = mybir.dt.float8_e4m3fn_x4
ALU = mybir.AluOpType
ACT = mybir.ActivationFunctionType

P = 128
PACK = 4
SIXTEENTH = 0.0625
HALF = S // 2
HALVES = (slice(0, HALF), slice(HALF, S))


def tile_picked_ringfdifkindd_none_p_kernel(tc, x_words, x_scales, d_words, d_scales, gs, tab, offs, k1, n1, n2, n3, n4, out):
    nc = tc.nc
    with ExitStack() as ctx:
        lists = ctx.enter_context(tc.tile_pool(name="lists", bufs=1))
        sb = ctx.enter_context(tc.tile_pool(name="sb", bufs=1))
        ps = ctx.enter_context(tc.psum_pool(name="ps", bufs=1))

        def load_list(src, name):
            tile = lists.tile([P, S // 16], U16, name=name)
            nc.sync.dma_start(tile[:], src)
            return tile

        def entries(tile, cols):
            return tile[:, cols.start // 16 : cols.stop // 16]

        def sbuf(shape, dtype, name, tag=None):
            return sb.tile(shape, dtype, name=name, tag=tag or name, align_bytes=64)

        xs_win = sbuf([P, T], U8, "xs_win")
        ds_plane = sbuf([P, H], U8, "ds_plane")
        nc.gpsimd.memset(xs_win[:].bitcast(I32), 0)
        nc.gpsimd.memset(ds_plane[:].bitcast(I32), 0)

        k1_t = load_list(k1, "k1_t")
        ds_win = sbuf([P, G], U8, "ds_win")
        nc.sync.dma_start(
            ds_win[:].bitcast(I32), d_scales[0].bitcast(I32).unsqueeze(1).broadcast_to([16, 8, G // 4])
        )
        gs_t = sbuf([P, PACK], F32, "gs_t")
        nc.scalar.dma_start(gs_t[:], gs.rearrange("(p t) o -> p (t o)", t=PACK))
        xs_rows = x_scales[0].bitcast(I32)
        for q in range(4):
            nc.scalar.dma_start(xs_win[:].bitcast(I32)[32 * q : 32 * q + 4, :], xs_rows[4 * q : 4 * q + 4, :])
        dw_win = sbuf([P, G], I32, "dw_win")
        nc.sync.dma_start(dw_win[:], d_words[0].rearrange("p n t -> p (n t)").bitcast(I32))
        offs_t = load_list(offs, "offs_t")
        xw_win = sbuf([P, T], I32, "xw_win")
        nc.sync.dma_start(xw_win[:], x_words[0].rearrange("p n t -> p (n t)").bitcast(I32))
        n1_t = load_list(n1, "n1_t")
        n2_t = load_list(n2, "n2_t")
        n3_t = load_list(n3, "n3_t")
        n4_t = load_list(n4, "n4_t")

        gs16 = sbuf([P, PACK], F32, "gs16")
        nc.scalar.activation(gs16[:], gs_t[:], ACT.Copy, scale=SIXTEENTH)
        gs_safe = sbuf([P, PACK], F32, "gs_safe")
        gs_inv = sbuf([P, PACK], F32, "gs_inv")

        ds_got = sbuf([P, H], U8, "ds_got")
        nc.vector.tensor_copy(ds_got[:], ds_win[:].indirect(k1_t[:]))
        nc.vector.scalar_tensor_tensor(gs_safe[:], gs_t[:], 0.0, gs_t[:], ALU.is_equal, ALU.subtract)
        ds_dealt = sbuf([P, H], U8, "ds_dealt")
        nc.vector.tensor_copy(
            ds_dealt[:].rearrange("p (t c i) -> p c t i", t=PACK, i=16),
            ds_got[:].rearrange("p (c i t) -> p c t i", t=PACK, i=16),
        )
        for a in range(4):
            nc.scalar.dma_start(ds_plane[:].bitcast(I32)[a:P:32, :], ds_dealt[:].bitcast(I32)[8 * a : P : 32, :])
        nc.vector.reciprocal(gs_inv[:], gs_safe[:])

        dw_got = sbuf([P, H], I32, "dw_got")
        nc.vector.tensor_copy(dw_got[:].bitcast(U32), dw_win[:].bitcast(U32).indirect(k1_t[:]))
        dw_dealt = sbuf([P, H], I32, "dw_dealt")
        nc.vector.tensor_copy(
            dw_dealt[:].rearrange("p (t c i) -> p c t i", t=PACK, i=4),
            dw_got[:].rearrange("p (c i t) -> p c t i", t=PACK, i=4),
        )
        xs_got = sbuf([P, S], U8, "xs_got")
        nc.vector.tensor_copy(xs_got[:], xs_win[:].indirect(offs_t[:]))
        xw_got = sbuf([P, S], I32, "xw_got")
        for cols in HALVES:
            nc.vector.tensor_copy(
                xw_got[:, cols].bitcast(U32), xw_win[:].bitcast(U32).indirect(entries(offs_t, cols))
            )

        tab_rows = tab.rearrange("(p t) j -> p t j", t=PACK)
        tab_win = []
        for t, slot in enumerate(("ds_got", "dw_got", "xs_win", "xw_win")):
            tile = sbuf([P, J], F32, "tab_win%d" % t, tag=slot)
            nc.sync.dma_start(tile[:], tab_rows[:, t, :])
            tab_win.append(tile)

        def product(bank, t, codes, scales):
            rows = slice(t * P, (t + 1) * P)
            nc.tensor.matmul_mx(
                out=bank,
                lhsT=dw_dealt[:, rows].bitcast(FP8X4),
                lhsT_scale=ds_plane[:, rows],
                rhs=codes.bitcast(FP8X4),
                rhs_scale=scales,
                start=True,
                stop=True,
            )

        early, late = (0, 1), (2, 3)
        banks = {(t, u): ps.tile([P, HALF], F32, name="bank%d%d" % (t, u))[:] for t in early for u in range(2)}
        whole_bank = {t: ps.tile([P, S], F32, name="bank%d" % t) for t in late}
        for t in late:
            for u, cols in enumerate(HALVES):
                banks[t, u] = whole_bank[t][:, cols]
        rows_win = [sbuf([P, 2 * S], F32, "rows_win%d" % t) for t in range(PACK)]
        for t in range(PACK):
            nc.gpsimd.memset(rows_win[t][:, S:], 0.0)

        for u, cols in enumerate(HALVES):
            for t in early:
                product(banks[t, u], t, xw_got[:, cols], xs_got[:, cols])
                nc.scalar.activation(rows_win[t][:, cols], banks[t, u], ACT.Copy, scale=gs16[:, t : t + 1])
        for t in late:
            product(whole_bank[t][:], t, xw_got[:], xs_got[:])
            nc.scalar.activation(rows_win[t][:, 0:S], whole_bank[t][:], ACT.Copy, scale=gs16[:, t : t + 1])

        near = sbuf([P, PACK, HALF], F32, "near")
        diff = [sbuf([P, PACK, HALF], F32, "diff%d" % u) for u in range(2)]
        bend = [sbuf([P, PACK, HALF], F32, "bend%d" % u) for u in range(2)]
        other = [sbuf([P, PACK, HALF], F32, "other%d" % u) for u in range(2)]
        steps = [(u, t) for u in range(2) for t in range(PACK)]

        def fetch_near(u, t):
            nc.vector.tensor_copy(near[:, t, :], rows_win[t][:].indirect(entries(n1_t, HALVES[u])))

        fetch_near(*steps[0])
        for step, (u, t) in enumerate(steps):
            if step + 1 < len(steps):
                fetch_near(*steps[step + 1])
            nc.vector.scalar_tensor_tensor(
                diff[u][:, t, :], banks[t, u], gs16[:, t : t + 1], near[:, t, :], ALU.mult, ALU.subtract
            )
            nc.scalar.activation(other[u][:, t, :], rows_win[t][:].indirect(entries(n2_t, HALVES[u])), ACT.Copy)
            nc.scalar.activation(bend[u][:, t, :], diff[u][:, t, :], ACT.Tanh, scale=gs_inv[:, t : t + 1])

        def fetch_kinds(t, u, into):
            nc.scalar.activation(into, tab_win[t][:].indirect(entries(n3_t, HALVES[u])), ACT.Copy)

        kinds1 = (diff[1][:, 3, :], other[1][:, 0, :])
        for u, cols in enumerate(HALVES):
            z = sbuf([P, HALF, PACK], BF16, "z%d" % u, tag=("near", "z1")[u])
            z_codes = sbuf([P, HALF], U32, "z_codes%d" % u)
            z_scales = sbuf([P, HALF], U8, "z_scales%d" % u)
            quarters = (slice(0, HALF // 2), slice(HALF // 2, HALF))
            for part in quarters:
                nc.vector.tensor_tensor(
                    z[:, part, :].rearrange("p (c i) t -> p c t i", i=4),
                    bend[u][:, :, part].rearrange("p t (c i) -> p c t i", i=4),
                    other[u][:, :, part].rearrange("p t (c i) -> p c t i", i=4),
                    ALU.mult,
                )
            for part in quarters:
                nc.vector.quantize_mx(
                    out=z_codes[:, part].bitcast(FP8X4),
                    scales=z_scales[:, part],
                    in_=z[:, part, :].rearrange("p c t -> p (c t)"),
                )
            fetch_kinds(1, u, kinds1[u])
            for t in range(PACK):
                product(banks[t, u], t, z_codes[:], z_scales[:])
                nc.scalar.activation(rows_win[t][:, cols], banks[t, u], ACT.Copy, scale=SIXTEENTH)

        first, second = HALVES
        whole = slice(0, S)
        kinds0 = sbuf([P, S], F32, "kinds0")
        rest = [sbuf([P, S], F32, "rest%d" % t) for t in range(PACK)]
        total = [sbuf([P, S], F32, "total%d" % t) for t in range(PACK)]
        size = [sbuf([P, S], F32, "size%d" % t) for t in range(PACK)]
        out_rows = out.rearrange("(p t) j -> p t j", t=PACK)

        def less_h2(t, cols, kinds):
            nc.vector.tensor_tensor(rest[t][:, cols], kinds, rows_win[t][:, cols], ALU.subtract)

        def add_far(t, cols):
            nc.vector.tensor_tensor(
                total[t][:, cols], rows_win[t][:].indirect(entries(n4_t, cols)), rest[t][:, cols], ALU.add
            )

        def finish(t, cols):
            nc.scalar.activation(size[t][:, cols], total[t][:, cols], ACT.Abs)
            nc.sync.dma_start(out_rows[:, t, cols], size[t][:, cols])

        for cols in HALVES:
            nc.vector.tensor_copy(kinds0[:, cols], tab_win[0][:].indirect(entries(n3_t, cols)))
        less_h2(0, first, kinds0[:, first])
        less_h2(1, first, kinds1[0])
        nc.vector.tensor_tensor(
            rest[2][:, first], tab_win[2][:].indirect(entries(n3_t, first)), rows_win[2][:, first], ALU.subtract
        )
        less_h2(0, second, kinds0[:, second])
        less_h2(1, second, kinds1[1])
        fetch_kinds(2, 1, kinds0[:, second])
        fetch_kinds(3, 0, kinds1[1])
        add_far(0, whole)
        fetch_kinds(3, 1, rest[0][:, first])
        far2 = sbuf([P, S], F32, "far2")
        nc.scalar.activation(far2[:], rows_win[2][:].indirect(n4_t[:]), ACT.Copy)
        finish(0, whole)
        less_h2(2, second, kinds0[:, second])
        less_h2(3, first, kinds1[1])
        add_far(1, whole)
        finish(1, whole)
        less_h2(3, second, rest[0][:, first])
        nc.vector.tensor_tensor(total[2][:], far2[:], rest[2][:], ALU.add)
        finish(2, whole)
        for cols in HALVES:
            add_far(3, cols)
            finish(3, cols)
